import numpy as np
import ml_dtypes


def mxq(x, axis, fmt="e4m3"):
    dtype, down = {"e4m3": (ml_dtypes.float8_e4m3fn, 7), "e5m2": (ml_dtypes.float8_e5m2, 14)}[fmt]
    v = np.moveaxis(np.asarray(x, np.float32).astype(ml_dtypes.bfloat16).astype(np.float64), axis, -1)
    blocks = v.reshape(v.shape[:-1] + (-1, 32))
    amax = np.abs(blocks).max(-1, keepdims=True)
    byte = np.maximum(np.where(amax > 0, np.frexp(amax)[1] - 1 + 127, 0) - down, 1)
    scale = np.exp2(byte - 127.0)
    codes = (blocks / scale).astype(np.float32).astype(dtype).astype(np.float64)
    return np.moveaxis((codes * scale).reshape(v.shape), -1, axis)


WIDE = False


def mx_kscale(k):
    if not WIDE:
        return np.ones(k)
    levels = np.array([10, -10, 5, -5, 0])
    if k % 512:
        return np.exp2(np.random.permutation(np.resize(levels, k // 32))).repeat(32)
    a = np.empty((k // 512, 16))
    for p in range(k // 512):
        a[p, :8] = np.random.permutation(np.resize(levels, 8))
        for g in range(8):
            far = levels[np.abs(levels - a[p, g]) >= 10]
            a[p, g + 8] = far[np.random.randint(len(far))]
    return np.exp2(a.ravel()).repeat(32)


def f64(x):
    return np.asarray(x).astype(np.float64)


E2M1 = np.array([0.0, 0.5, 1.0, 1.5, 2.0, 3.0, 4.0, 6.0, -0.0, -0.5, -1.0, -1.5, -2.0, -3.0, -4.0, -6.0])


def pack_weight(w, fmt):
    k, n = w.shape
    w = f64(np.asarray(w, np.float32).astype(ml_dtypes.bfloat16)).reshape(k // 32, 32, n)
    amax = np.abs(w).max(1)
    if fmt == "e4m3":
        byte = np.frexp(amax)[1] - 1 + 127 - 7
    else:
        mant, ex = np.frexp(amax / 6.0)
        byte = np.where(mant > 0.5, ex, ex - 1) + 127
    byte = np.clip(np.where(amax > 0, byte, 1), 1, 254)
    scaled = (w * np.exp2(127.0 - byte)[:, None, :]).reshape(k, n).astype(np.float32)
    by_word = np.ascontiguousarray(scaled.reshape(k // 512, 128, 4, n).transpose(0, 1, 3, 2))
    if fmt == "e4m3":
        words = by_word.astype(ml_dtypes.float8_e4m3fn).view(np.uint8)
    else:
        c = by_word.astype(ml_dtypes.float4_e2m1fn).view(np.uint8) & 0xF
        words = (c[..., 0::2] | (c[..., 1::2] << 4)).reshape(k // 512, 128, 2 * n)
    return np.ascontiguousarray(words), np.ascontiguousarray(byte.astype(np.uint8).reshape(k // 512, 16, n))


def unpack_weight(words, scales, fmt):
    g, _, n = scales.shape
    words = np.ascontiguousarray(words).reshape(g, 128, n, -1)
    if fmt == "e4m3":
        vals = words.view(ml_dtypes.float8_e4m3fn).astype(np.float64)
    else:
        nib = np.empty((g, 128, n, 4), np.uint8)
        nib[..., 0::2] = words & 0xF
        nib[..., 1::2] = words >> 4
        vals = E2M1[nib]
    vals = vals * np.repeat(np.exp2(scales.astype(np.float64) - 127.0), 8, axis=1)[..., None]
    return vals.transpose(0, 1, 3, 2).reshape(g * 512, n)


def planes(y):
    n, m = y.shape
    v = y.astype(np.float32).astype(ml_dtypes.bfloat16).astype(np.float64).reshape(n // 32, 32, m)
    top = np.abs(v).max(1)
    byte = np.clip(np.where(top > 0, np.frexp(top)[1] - 1 + 127 - 7, 1), 1, 254)
    codes = (v * np.exp2(127.0 - byte)[:, None, :]).reshape(n, m).astype(np.float32).astype(ml_dtypes.float8_e4m3fn).view(np.uint8)
    words = codes.reshape(n // 512, 128, 4, m).transpose(0, 1, 3, 2)
    return np.ascontiguousarray(words), np.ascontiguousarray(byte.astype(np.uint8).reshape(n // 512, 16, m))


def gelu(v):
    return 0.5 * v * (1.0 + np.tanh(np.sqrt(2.0 / np.pi) * (v + 0.044715 * v**3)))


K, M, T = 2048, 1024, 512


def setup_inputs():
    n = np.random.standard_normal
    s = mx_kscale(K)[:, None]
    p_w4 = pack_weight(n((K, M)) / np.sqrt(K) / s ** 2, "e2m1")
    p_w8 = pack_weight(n((K, M)) / np.sqrt(K) / s, "e4m3")
    return {
        "x": (n((K, T)) * s).astype(np.float32),
        "w4_words": p_w4[0],
        "w4_scales": p_w4[1],
        "w8_words": p_w8[0],
        "w8_scales": p_w8[1],
        "b": (0.3 * n(1024)).astype(np.float32),
    }


def reference(x, w4_words, w4_scales, w8_words, w8_scales, b):
    xa_, xb_ = mxq(f64(x) ** 2, 0, "e4m3"), mxq(f64(x), 0, "e4m3")
    w4_ = unpack_weight(w4_words, w4_scales, "e2m1")
    w8_ = unpack_weight(w8_words, w8_scales, "e4m3")
    y = xa_.T @ w4_ + xb_.T @ w8_
    out_0 = gelu(y + f64(b)[None, :])
    return (out_0,) + planes(out_0)

@@ -1,0 +1,244 @@
+from contextlib import ExitStack
+
+import concourse.mybir as mybir
+from concourse.masks import make_identity
+
+K, M, T = 2048, 1024, 512
+FLOPS = 2 * 2 * K * M * T
+
+F32 = mybir.dt.float32
+BF16 = mybir.dt.bfloat16
+U32 = mybir.dt.uint32
+I32 = mybir.dt.int32
+U8 = mybir.dt.uint8
+FP8X4 = mybir.dt.float8_e4m3fn_x4
+FP4X4 = mybir.dt.float4_e2m1fn_x4
+ACT = mybir.ActivationFunctionType
+ALU = mybir.AluOpType
+
+P = 128
+PACK = 4
+PASSES = K // (P * PACK)
+HALF = 512
+HALVES = M // HALF
+CHUNKS = 2
+TC = T // CHUNKS
+MC = TC // PACK
+
+
+def tile_mix_feat_tm_quadpl_gelu_kernel(tc, x, w4_words, w4_scales, w8_words, w8_scales, b, out_0, out_1, out_2):
+    nc = tc.nc
+    with ExitStack() as ctx:
+        keep = ctx.enter_context(tc.tile_pool(name="keep", bufs=1))
+        psum = ctx.enter_context(tc.psum_pool(name="psum", bufs=1))
+        ctx.enter_context(tc.manual_schedule())
+
+        x_raw = {(a, c): keep.tile([P, PACK, TC], F32, name="x_raw_%d_%d" % (a, c), align_bytes=64) for a in range(PASSES) for c in range(CHUNKS)}
+        w8 = {(a, h): keep.tile([P, HALF], U32, name="w8_%d_%d" % (a, h), align_bytes=64) for a in range(PASSES) for h in range(HALVES)}
+        w4 = {a: keep.tile([P, 2 * M], U8, name="w4_%d" % a, align_bytes=64) for a in range(PASSES)}
+        s8 = keep.tile([P, M], U8, align_bytes=64)
+        s4 = keep.tile([P, PASSES, M], U8, align_bytes=64)
+        grouped = {(f, a): keep.tile([P, PACK, P, PACK], BF16, name="grouped_%s_%d" % (f, a), align_bytes=64) for f in "ab" for a in range(PASSES)}
+        codes = {(f, a): keep.tile([P, T], U32, name="codes_%s_%d" % (f, a), align_bytes=64) for f in "ab" for a in range(PASSES)}
+        scales = {(f, a): keep.tile([P, T], U8, name="scales_%s_%d" % (f, a), align_bytes=64) for f in "ab" for a in range(PASSES)}
+        ident = keep.tile([P, P], F32, align_bytes=64)
+        b_rows = keep.tile([P, 8], F32, align_bytes=64)
+        bias = keep.tile([P, M], F32, align_bytes=64)
+        warm_in = keep.tile([P, 1], F32)
+        warm_out = keep.tile([P, 1], F32)
+        pre = {(h, i): keep.tile([P, HALF], F32, name="pre_%d_%d" % (h, i), align_bytes=64) for h in range(HALVES) for i in range(PACK)}
+        res = {h: keep.tile([P, PACK, HALF], F32, name="res_%d" % h, align_bytes=64) for h in range(HALVES)}
+        res_grouped = {h: keep.tile([P, HALF, PACK], BF16, name="res_grouped_%d" % h, align_bytes=64) for h in range(HALVES)}
+        res_codes = {h: keep.tile([P, HALF], U32, name="res_codes_%d" % h, align_bytes=64) for h in range(HALVES)}
+        res_scales = keep.tile([P, M], U8, align_bytes=64)
+
+        def load_x(a):
+            rows = x[a * P * PACK:(a + 1) * P * PACK, :].rearrange("(p j) t -> p j t", j=PACK)
+            for c in range(CHUNKS):
+                nc.sync.dma_start(out=x_raw[a, c][:], in_=rows[:, :, c * TC:(c + 1) * TC])
+
+        def load_w8(a, h):
+            src = w8_words[a].rearrange("p n i -> p (n i)")[:, h * HALF * PACK:(h + 1) * HALF * PACK]
+            nc.sync.dma_start(out=w8[a, h][:].bitcast(I32), in_=src.bitcast(I32))
+
+        def load_w4(a, h0, h1):
+            cols = slice(2 * HALF * h0, 2 * HALF * h1)
+            nc.sync.dma_start(out=w4[a][:, cols].bitcast(I32), in_=w4_words[a][:, cols].bitcast(I32))
+
+        def load_s8():
+            for q in (0, 2, 1, 3):
+                nc.sync.dma_start(out=s8[32 * q:32 * q + 16, :].bitcast(I32), in_=w8_scales[:, 4 * q:4 * q + 4, :].bitcast(I32))
+
+        def load_s4():
+            rows = w4_scales.rearrange("a (q r) n -> r q a n", r=4)
+            for r in range(4):
+                nc.sync.dma_start(out=s4[r:P:32, :, :].bitcast(I32), in_=rows[r].bitcast(I32))
+
+        def group_views(f, a, c):
+            dst = grouped[f, a][:, :, c * MC:(c + 1) * MC, :].rearrange("p r m j -> p m r j")
+            src = x_raw[a, c][:].rearrange("p j (m r) -> p m r j", r=PACK)
+            return dst, src
+
+        def group_b(a, c):
+            dst, src = group_views("b", a, c)
+            nc.vector.tensor_copy(out=dst, in_=src)
+
+        def group_a(a, c):
+            dst, src = group_views("a", a, c)
+            nc.scalar.activation(out=dst, in_=src, func=ACT.Square)
+
+        def quantize(f, a, r0, r1):
+            cols = slice(r0 * P, r1 * P)
+            nc.vector.quantize_mx(
+                out=codes[f, a][:, cols].bitcast(FP8X4),
+                scales=scales[f, a][:, cols],
+                in_=grouped[f, a][:, r0:r1, :, :].rearrange("p r m j -> p (r m j)"),
+            )
+
+        acc = {}
+        done = {}
+
+        def mm(f, a, h, i):
+            if (h, i) not in acc:
+                acc[h, i] = psum.tile([P, HALF], F32, name="acc_%d_%d" % (h, i), tag="bank_%d_%d" % (h, i))
+                done[h, i] = 0
+            cols = slice(i * P, (i + 1) * P)
+            ncols = slice(h * HALF, (h + 1) * HALF)
+            if f == "b":
+                rhs = w8[a, h][:].bitcast(FP8X4)
+                rhs_scale = s8[4 * a:, ncols]
+            else:
+                rhs = w4[a][:, 2 * h * HALF:2 * (h + 1) * HALF].bitcast(FP4X4)
+                rhs_scale = s4[:, a, ncols]
+            nc.tensor.matmul_mx(
+                out=acc[h, i][:],
+                lhsT=codes[f, a][:, cols].bitcast(FP8X4),
+                lhsT_scale=scales[f, a][:, cols],
+                rhs=rhs,
+                rhs_scale=rhs_scale,
+                start=(done[h, i] == 0),
+                stop=(done[h, i] == 2 * PASSES - 1),
+            )
+            done[h, i] += 1
+
+        def unit(f, a, h):
+            for i in range(PACK):
+                mm(f, a, h, i)
+
+        out_rows = out_0.rearrange("(p i) n -> p i n", i=PACK)
+
+        def add_bias(h, i, c0, c1):
+            nc.vector.tensor_tensor(out=pre[h, i][:, c0:c1], in0=acc[h, i][:, c0:c1], in1=bias[:, h * HALF + c0:h * HALF + c1], op=ALU.add)
+
+        def gelu(h, i, c0, c1):
+            nc.scalar.activation(out=res[h][:, i, c0:c1], in_=pre[h, i][:, c0:c1], func=ACT.Gelu_apprx_tanh)
+
+        def store_res(h, i):
+            nc.sync.dma_start(out=out_rows[:, i, h * HALF:(h + 1) * HALF], in_=res[h][:, i, :])
+
+        def group_res(h, c0, c1, on_vector):
+            dst = res_grouped[h][:, c0:c1, :]
+            src = res[h][:, :, c0:c1].rearrange("p i n -> p n i")
+            if on_vector:
+                nc.vector.tensor_copy(out=dst, in_=src)
+            else:
+                nc.scalar.copy(out=dst, in_=src)
+
+        def quantize_res(h, c0, c1):
+            nc.vector.quantize_mx(
+                out=res_codes[h][:, c0:c1].bitcast(FP8X4),
+                scales=res_scales[:, h * HALF + c0:h * HALF + c1],
+                in_=res_grouped[h][:, c0:c1, :].rearrange("p n i -> p (n i)"),
+            )
+
+        def store_codes(h, c0, c1):
+            dst = out_1[0].rearrange("p n i -> p (n i)")[:, (h * HALF + c0) * PACK:(h * HALF + c1) * PACK]
+            nc.sync.dma_start(out=dst.bitcast(I32), in_=res_codes[h][:, c0:c1].bitcast(I32))
+
+        def store_scales(q, queue):
+            queue.dma_start(out=out_2[0, 4 * q:4 * q + 4, :].bitcast(I32), in_=res_scales[32 * q:32 * q + 4, :].bitcast(I32))
+
+        nc.scalar.dma_start(out=b_rows[:], in_=b.rearrange("(p c) -> p c", c=8))
+        nc.vector.memset(warm_in[:], 0.0)
+        nc.vector.memset(s8[:].bitcast(I32), 0)
+        nc.vector.memset(s4[:].rearrange("p a n -> p (a n)").bitcast(I32), 0)
+        nc.scalar.activation(out=warm_out[:], in_=warm_in[:], func=ACT.Gelu_apprx_tanh)
+        make_identity(nc, ident[:])
+
+        load_x(0)
+        load_s8()
+        load_w8(0, 0)
+        load_s4()
+        load_w4(0, 0, 2)
+        for a in range(1, PASSES):
+            load_x(a)
+            load_w8(a, 0)
+            load_w4(a, 0, 2)
+        for a in range(PASSES):
+            load_w8(a, 1)
+
+        bias_banks = []
+        for g in range(2):
+            bank = psum.tile([P, 4, P], F32, name="bias_bank_%d" % g, tag="bank_1_%d" % (2 + g))
+            for c in range(4):
+                col = 4 * g + c
+                nc.tensor.transpose(bank[:, c, :], b_rows[:, col:col + 1].to_broadcast([P, P]), ident[:])
+            bias_banks.append(bank)
+
+        for a in range(PASSES):
+            for c in range(CHUNKS):
+                group_b(a, c)
+                group_a(a, c)
+            if a == 0:
+                for g in range(2):
+                    nc.scalar.copy(
+                        out=bias[:].rearrange("p (n g c) -> p n g c", g=2, c=4)[:, :, g, :],
+                        in_=bias_banks[g][:].rearrange("p c n -> p n c"),
+                    )
+            quantize("b", a, 0, 1)
+            quantize("b", a, 1, 2)
+            quantize("b", a, 2, 4)
+            quantize("a", a, 0, 2)
+            quantize("a", a, 2, 4)
+            unit("b", a, 0)
+            unit("a", a, 0)
+            if a < PASSES - 1:
+                unit("a", a, 1)
+        for i in range(PACK):
+            for a in range(PASSES):
+                mm("b", a, 1, i)
+            mm("a", PASSES - 1, 1, i)
+
+        for i in range(PACK):
+            add_bias(0, i, 0, HALF)
+            gelu(0, i, 0, HALF)
+            store_res(0, i)
+        add_bias(1, 0, 0, HALF)
+        gelu(1, 0, 0, HALF)
+        store_res(1, 0)
+        group_res(0, 0, 256, True)
+        group_res(0, 256, 512, True)
+        add_bias(1, 1, 0, HALF)
+        gelu(1, 1, 0, HALF)
+        store_res(1, 1)
+        quantize_res(0, 0, HALF)
+        store_codes(0, 0, HALF)
+        add_bias(1, 2, 0, HALF)
+        gelu(1, 2, 0, HALF)
+        store_res(1, 2)
+        add_bias(1, 3, 0, 256)
+        add_bias(1, 3, 256, 512)
+        gelu(1, 3, 0, 256)
+        gelu(1, 3, 256, 512)
+        store_res(1, 3)
+        group_res(1, 0, 256, True)
+        group_res(1, 256, 384, True)
+        group_res(1, 384, 512, False)
+        quantize_res(1, 0, 256)
+        store_codes(1, 0, 256)
+        quantize_res(1, 256, 512)
+        store_codes(1, 256, 512)
+        store_scales(0, nc.scalar)
+        store_scales(2, nc.scalar)
+        store_scales(1, nc.sync)
+        store_scales(3, nc.sync)

@@ -22,8 +22,6 @@ PASSES = K // (P * PACK)
 HALF = 512
 HALVES = M // HALF
 CHUNKS = 2
-TC = T // CHUNKS
-MC = TC // PACK
 
 
 def tile_mix_feat_tm_quadpl_gelu_kernel(tc, x, w4_words, w4_scales, w8_words, w8_scales, b, out_0, out_1, out_2):
@@ -33,7 +31,7 @@ def tile_mix_feat_tm_quadpl_gelu_kernel(tc, x, w4_words, w4_scales, w8_words, w8
         psum = ctx.enter_context(tc.psum_pool(name="psum", bufs=1))
         ctx.enter_context(tc.manual_schedule())
 
-        x_raw = {(a, c): keep.tile([P, PACK, TC], F32, name="x_raw_%d_%d" % (a, c), align_bytes=64) for a in range(PASSES) for c in range(CHUNKS)}
+        x_raw = {a: keep.tile([P, PACK, T], F32, name="x_raw_%d" % a, align_bytes=64) for a in range(PASSES)}
         w8 = {(a, h): keep.tile([P, HALF], U32, name="w8_%d_%d" % (a, h), align_bytes=64) for a in range(PASSES) for h in range(HALVES)}
         w4 = {a: keep.tile([P, 2 * M], U8, name="w4_%d" % a, align_bytes=64) for a in range(PASSES)}
         s8 = keep.tile([P, M], U8, align_bytes=64)
@@ -54,8 +52,7 @@ def tile_mix_feat_tm_quadpl_gelu_kernel(tc, x, w4_words, w4_scales, w8_words, w8
 
         def load_x(a):
             rows = x[a * P * PACK:(a + 1) * P * PACK, :].rearrange("(p j) t -> p j t", j=PACK)
-            for c in range(CHUNKS):
-                nc.sync.dma_start(out=x_raw[a, c][:], in_=rows[:, :, c * TC:(c + 1) * TC])
+            nc.sync.dma_start(out=x_raw[a][:], in_=rows)
 
         def load_w8(a, h):
             src = w8_words[a].rearrange("p n i -> p (n i)")[:, h * HALF * PACK:(h + 1) * HALF * PACK]
@@ -75,8 +72,8 @@ def tile_mix_feat_tm_quadpl_gelu_kernel(tc, x, w4_words, w4_scales, w8_words, w8
                 nc.sync.dma_start(out=s4[r:P:32, :, :].bitcast(I32), in_=rows[r].bitcast(I32))
 
         def group_views(f, a, c):
-            dst = grouped[f, a][:, :, c * MC:(c + 1) * MC, :].rearrange("p r m j -> p m r j")
-            src = x_raw[a, c][:].rearrange("p j (m r) -> p m r j", r=PACK)
+            dst = grouped[f, a][:, 2 * c:2 * c + 2, :, :].rearrange("p r m j -> p m j r")
+            src = x_raw[a][:].rearrange("p j (m r) -> p m j r", r=PACK)[:, :, :, 2 * c:2 * c + 2]
             return dst, src
 
         def group_b(a, c):
@@ -137,8 +134,8 @@ def tile_mix_feat_tm_quadpl_gelu_kernel(tc, x, w4_words, w4_scales, w8_words, w8
             nc.sync.dma_start(out=out_rows[:, i, h * HALF:(h + 1) * HALF], in_=res[h][:, i, :])
 
         def group_res(h, c0, c1, on_vector):
-            dst = res_grouped[h][:, c0:c1, :]
-            src = res[h][:, :, c0:c1].rearrange("p i n -> p n i")
+            dst = res_grouped[h][:, c0:c1, :].rearrange("p (c u) i -> p c i u", u=4)
+            src = res[h][:, :, c0:c1].rearrange("p i (c u) -> p c i u", u=4)
             if on_vector:
                 nc.vector.tensor_copy(out=dst, in_=src)
             else:
@@ -158,7 +155,7 @@ def tile_mix_feat_tm_quadpl_gelu_kernel(tc, x, w4_words, w4_scales, w8_words, w8
         def store_scales(q, queue):
             queue.dma_start(out=out_2[0, 4 * q:4 * q + 4, :].bitcast(I32), in_=res_scales[32 * q:32 * q + 4, :].bitcast(I32))
 
-        nc.scalar.dma_start(out=b_rows[:], in_=b.rearrange("(p c) -> p c", c=8))
+        nc.sync.dma_start(out=b_rows[:], in_=b.rearrange("(p c) -> p c", c=8))
         nc.vector.memset(warm_in[:], 0.0)
         nc.vector.memset(s8[:].bitcast(I32), 0)
         nc.vector.memset(s4[:].rearrange("p a n -> p (a n)").bitcast(I32), 0)
@@ -189,25 +186,21 @@ def tile_mix_feat_tm_quadpl_gelu_kernel(tc, x, w4_words, w4_scales, w8_words, w8
             for c in range(CHUNKS):
                 group_b(a, c)
                 group_a(a, c)
+                quantize("b", a, 2 * c, 2 * c + 2)
             if a == 0:
                 for g in range(2):
                     nc.scalar.copy(
                         out=bias[:].rearrange("p (n g c) -> p n g c", g=2, c=4)[:, :, g, :],
                         in_=bias_banks[g][:].rearrange("p c n -> p n c"),
                     )
-            quantize("b", a, 0, 1)
-            quantize("b", a, 1, 2)
-            quantize("b", a, 2, 4)
             quantize("a", a, 0, 2)
             quantize("a", a, 2, 4)
             unit("b", a, 0)
             unit("a", a, 0)
-            if a < PASSES - 1:
-                unit("a", a, 1)
+            unit("a", a, 1)
         for i in range(PACK):
             for a in range(PASSES):
                 mm("b", a, 1, i)
-            mm("a", PASSES - 1, 1, i)
 
         for i in range(PACK):
             add_bias(0, i, 0, HALF)
@@ -226,14 +219,17 @@ def tile_mix_feat_tm_quadpl_gelu_kernel(tc, x, w4_words, w4_scales, w8_words, w8
         add_bias(1, 2, 0, HALF)
         gelu(1, 2, 0, HALF)
         store_res(1, 2)
-        add_bias(1, 3, 0, 256)
+        add_bias(1, 3, 0, 128)
+        add_bias(1, 3, 128, 256)
         add_bias(1, 3, 256, 512)
-        gelu(1, 3, 0, 256)
+        gelu(1, 3, 0, 128)
+        gelu(1, 3, 128, 256)
         gelu(1, 3, 256, 512)
         store_res(1, 3)
-        group_res(1, 0, 256, True)
-        group_res(1, 256, 384, True)
+        group_res(1, 0, 128, True)
+        group_res(1, 128, 256, True)
         group_res(1, 384, 512, False)
+        group_res(1, 256, 384, True)
         quantize_res(1, 0, 256)
         store_codes(1, 0, 256)
         quantize_res(1, 256, 512)

@@ -34,8 +34,9 @@ def tile_mix_feat_tm_quadpl_gelu_kernel(tc, x, w4_words, w4_scales, w8_words, w8
         x_raw = {a: keep.tile([P, PACK, T], F32, name="x_raw_%d" % a, align_bytes=64) for a in range(PASSES)}
         w8 = {(a, h): keep.tile([P, HALF], U32, name="w8_%d_%d" % (a, h), align_bytes=64) for a in range(PASSES) for h in range(HALVES)}
         w4 = {a: keep.tile([P, 2 * M], U8, name="w4_%d" % a, align_bytes=64) for a in range(PASSES)}
-        s8 = keep.tile([P, M], U8, align_bytes=64)
-        s4 = keep.tile([P, PASSES, M], U8, align_bytes=64)
+        s8 = {h: keep.tile([P, HALF], U8, name="s8_%d" % h, align_bytes=64) for h in range(HALVES)}
+        s4_early = keep.tile([P, PASSES - 1, M], U8, align_bytes=64)
+        s4_last = keep.tile([P, 1, M], U8, align_bytes=64)
         grouped = {(f, a): keep.tile([P, PACK, P, PACK], BF16, name="grouped_%s_%d" % (f, a), align_bytes=64) for f in "ab" for a in range(PASSES)}
         codes = {(f, a): keep.tile([P, T], U32, name="codes_%s_%d" % (f, a), align_bytes=64) for f in "ab" for a in range(PASSES)}
         scales = {(f, a): keep.tile([P, T], U8, name="scales_%s_%d" % (f, a), align_bytes=64) for f in "ab" for a in range(PASSES)}
@@ -62,14 +63,15 @@ def tile_mix_feat_tm_quadpl_gelu_kernel(tc, x, w4_words, w4_scales, w8_words, w8
             cols = slice(2 * HALF * h0, 2 * HALF * h1)
             nc.sync.dma_start(out=w4[a][:, cols].bitcast(I32), in_=w4_words[a][:, cols].bitcast(I32))
 
-        def load_s8():
+        def load_s8(h):
             for q in (0, 2, 1, 3):
-                nc.sync.dma_start(out=s8[32 * q:32 * q + 16, :].bitcast(I32), in_=w8_scales[:, 4 * q:4 * q + 4, :].bitcast(I32))
+                src = w8_scales[:, 4 * q:4 * q + 4, h * HALF:(h + 1) * HALF]
+                nc.sync.dma_start(out=s8[h][32 * q:32 * q + 16, :].bitcast(I32), in_=src.bitcast(I32))
 
-        def load_s4():
+        def load_s4(plane, a0, a1):
             rows = w4_scales.rearrange("a (q r) n -> r q a n", r=4)
             for r in range(4):
-                nc.sync.dma_start(out=s4[r:P:32, :, :].bitcast(I32), in_=rows[r].bitcast(I32))
+                nc.sync.dma_start(out=plane[r:P:32, :, :].bitcast(I32), in_=rows[r][:, a0:a1, :].bitcast(I32))
 
         def group_views(f, a, c):
             dst = grouped[f, a][:, 2 * c:2 * c + 2, :, :].rearrange("p r m j -> p m j r")
@@ -103,10 +105,10 @@ def tile_mix_feat_tm_quadpl_gelu_kernel(tc, x, w4_words, w4_scales, w8_words, w8
             ncols = slice(h * HALF, (h + 1) * HALF)
             if f == "b":
                 rhs = w8[a, h][:].bitcast(FP8X4)
-                rhs_scale = s8[4 * a:, ncols]
+                rhs_scale = s8[h][4 * a:, :]
             else:
                 rhs = w4[a][:, 2 * h * HALF:2 * (h + 1) * HALF].bitcast(FP4X4)
-                rhs_scale = s4[:, a, ncols]
+                rhs_scale = s4_early[:, a, ncols] if a < PASSES - 1 else s4_last[:, 0, ncols]
             nc.tensor.matmul_mx(
                 out=acc[h, i][:],
                 lhsT=codes[f, a][:, cols].bitcast(FP8X4),
@@ -157,20 +159,25 @@ def tile_mix_feat_tm_quadpl_gelu_kernel(tc, x, w4_words, w4_scales, w8_words, w8
 
         nc.sync.dma_start(out=b_rows[:], in_=b.rearrange("(p c) -> p c", c=8))
         nc.vector.memset(warm_in[:], 0.0)
-        nc.vector.memset(s8[:].bitcast(I32), 0)
-        nc.vector.memset(s4[:].rearrange("p a n -> p (a n)").bitcast(I32), 0)
+        nc.vector.memset(s8[0][:].bitcast(I32), 0)
+        nc.vector.memset(s4_early[:].rearrange("p a n -> p (a n)").bitcast(I32), 0)
+        nc.vector.memset(s8[1][:].bitcast(I32), 0)
+        nc.vector.memset(s4_last[:].rearrange("p a n -> p (a n)").bitcast(I32), 0)
         nc.scalar.activation(out=warm_out[:], in_=warm_in[:], func=ACT.Gelu_apprx_tanh)
         make_identity(nc, ident[:])
 
         load_x(0)
-        load_s8()
+        load_s8(0)
         load_w8(0, 0)
-        load_s4()
+        load_s4(s4_early, 0, PASSES - 1)
         load_w4(0, 0, 2)
         for a in range(1, PASSES):
             load_x(a)
             load_w8(a, 0)
+            if a == PASSES - 1:
+                load_s4(s4_last, a, a + 1)
             load_w4(a, 0, 2)
+        load_s8(1)
         for a in range(PASSES):
             load_w8(a, 1)
 
@@ -182,22 +189,33 @@ def tile_mix_feat_tm_quadpl_gelu_kernel(tc, x, w4_words, w4_scales, w8_words, w8
                 nc.tensor.transpose(bank[:, c, :], b_rows[:, col:col + 1].to_broadcast([P, P]), ident[:])
             bias_banks.append(bank)
 
-        for a in range(PASSES):
+        def pair(f, a, h, c):
+            for i in (2 * c, 2 * c + 1):
+                mm(f, a, h, i)
+
+        for c in range(CHUNKS):
+            group_b(0, c)
+            group_a(0, c)
+            quantize("b", 0, 2 * c, 2 * c + 2)
+            pair("b", 0, 0, c)
+        for g in range(2):
+            nc.scalar.copy(
+                out=bias[:].rearrange("p (n g c) -> p n g c", g=2, c=4)[:, :, g, :],
+                in_=bias_banks[g][:].rearrange("p c n -> p n c"),
+            )
+        for c in range(CHUNKS):
+            quantize("a", 0, 2 * c, 2 * c + 2)
+            pair("a", 0, 0, c)
+            pair("a", 0, 1, c)
+        for a in range(1, PASSES):
             for c in range(CHUNKS):
                 group_b(a, c)
                 group_a(a, c)
                 quantize("b", a, 2 * c, 2 * c + 2)
-            if a == 0:
-                for g in range(2):
-                    nc.scalar.copy(
-                        out=bias[:].rearrange("p (n g c) -> p n g c", g=2, c=4)[:, :, g, :],
-                        in_=bias_banks[g][:].rearrange("p c n -> p n c"),
-                    )
-            quantize("a", a, 0, 2)
-            quantize("a", a, 2, 4)
-            unit("b", a, 0)
-            unit("a", a, 0)
-            unit("a", a, 1)
+                quantize("a", a, 2 * c, 2 * c + 2)
+                pair("b", a, 0, c)
+                pair("a", a, 0, c)
+                pair("a", a, 1, c)
         for i in range(PACK):
             for a in range(PASSES):
                 mm("b", a, 1, i)
@@ -206,18 +224,20 @@ def tile_mix_feat_tm_quadpl_gelu_kernel(tc, x, w4_words, w4_scales, w8_words, w8
             add_bias(0, i, 0, HALF)
             gelu(0, i, 0, HALF)
             store_res(0, i)
+        group_res(0, 384, 512, False)
         add_bias(1, 0, 0, HALF)
         gelu(1, 0, 0, HALF)
         store_res(1, 0)
         group_res(0, 0, 256, True)
-        group_res(0, 256, 512, True)
+        group_res(0, 256, 384, False)
         add_bias(1, 1, 0, HALF)
         gelu(1, 1, 0, HALF)
         store_res(1, 1)
-        quantize_res(0, 0, HALF)
-        store_codes(0, 0, HALF)
+        quantize_res(0, 0, 256)
         add_bias(1, 2, 0, HALF)
         gelu(1, 2, 0, HALF)
+        quantize_res(0, 256, 512)
+        store_codes(0, 0, HALF)
         store_res(1, 2)
         add_bias(1, 3, 0, 128)
         add_bias(1, 3, 128, 256)

@@ -43,8 +43,6 @@ def tile_mix_feat_tm_quadpl_gelu_kernel(tc, x, w4_words, w4_scales, w8_words, w8
         ident = keep.tile([P, P], F32, align_bytes=64)
         b_rows = keep.tile([P, 8], F32, align_bytes=64)
         bias = keep.tile([P, M], F32, align_bytes=64)
-        warm_in = keep.tile([P, 1], F32)
-        warm_out = keep.tile([P, 1], F32)
         pre = {(h, i): keep.tile([P, HALF], F32, name="pre_%d_%d" % (h, i), align_bytes=64) for h in range(HALVES) for i in range(PACK)}
         res = {h: keep.tile([P, PACK, HALF], F32, name="res_%d" % h, align_bytes=64) for h in range(HALVES)}
         res_grouped = {h: keep.tile([P, HALF, PACK], BF16, name="res_grouped_%d" % h, align_bytes=64) for h in range(HALVES)}
@@ -158,12 +156,10 @@ def tile_mix_feat_tm_quadpl_gelu_kernel(tc, x, w4_words, w4_scales, w8_words, w8
             queue.dma_start(out=out_2[0, 4 * q:4 * q + 4, :].bitcast(I32), in_=res_scales[32 * q:32 * q + 4, :].bitcast(I32))
 
         nc.sync.dma_start(out=b_rows[:], in_=b.rearrange("(p c) -> p c", c=8))
-        nc.vector.memset(warm_in[:], 0.0)
         nc.vector.memset(s8[0][:].bitcast(I32), 0)
         nc.vector.memset(s4_early[:].rearrange("p a n -> p (a n)").bitcast(I32), 0)
         nc.vector.memset(s8[1][:].bitcast(I32), 0)
         nc.vector.memset(s4_last[:].rearrange("p a n -> p (a n)").bitcast(I32), 0)
-        nc.scalar.activation(out=warm_out[:], in_=warm_in[:], func=ACT.Gelu_apprx_tanh)
         make_identity(nc, ident[:])
 
         load_x(0)

from contextlib import ExitStack

import concourse.mybir as mybir
from concourse.masks import make_identity

K, M, T = 2048, 1024, 512
FLOPS = 2 * 2 * K * M * T

F32 = mybir.dt.float32
BF16 = mybir.dt.bfloat16
U32 = mybir.dt.uint32
I32 = mybir.dt.int32
U8 = mybir.dt.uint8
FP8X4 = mybir.dt.float8_e4m3fn_x4
FP4X4 = mybir.dt.float4_e2m1fn_x4
ACT = mybir.ActivationFunctionType
ALU = mybir.AluOpType

P = 128
PACK = 4
PASSES = K // (P * PACK)
HALF = 512
HALVES = M // HALF
CHUNKS = 2


def tile_mix_feat_tm_quadpl_gelu_kernel(tc, x, w4_words, w4_scales, w8_words, w8_scales, b, out_0, out_1, out_2):
    nc = tc.nc
    with ExitStack() as ctx:
        keep = ctx.enter_context(tc.tile_pool(name="keep", bufs=1))
        psum = ctx.enter_context(tc.psum_pool(name="psum", bufs=1))
        ctx.enter_context(tc.manual_schedule())

        x_raw = {a: keep.tile([P, PACK, T], F32, name="x_raw_%d" % a, align_bytes=64) for a in range(PASSES)}
        w8 = {(a, h): keep.tile([P, HALF], U32, name="w8_%d_%d" % (a, h), align_bytes=64) for a in range(PASSES) for h in range(HALVES)}
        w4 = {a: keep.tile([P, 2 * M], U8, name="w4_%d" % a, align_bytes=64) for a in range(PASSES)}
        s8 = {h: keep.tile([P, HALF], U8, name="s8_%d" % h, align_bytes=64) for h in range(HALVES)}
        s4_early = keep.tile([P, PASSES - 1, M], U8, align_bytes=64)
        s4_last = keep.tile([P, 1, M], U8, align_bytes=64)
        grouped = {(f, a): keep.tile([P, PACK, P, PACK], BF16, name="grouped_%s_%d" % (f, a), align_bytes=64) for f in "ab" for a in range(PASSES)}
        codes = {(f, a): keep.tile([P, T], U32, name="codes_%s_%d" % (f, a), align_bytes=64) for f in "ab" for a in range(PASSES)}
        scales = {(f, a): keep.tile([P, T], U8, name="scales_%s_%d" % (f, a), align_bytes=64) for f in "ab" for a in range(PASSES)}
        ident = keep.tile([P, P], F32, align_bytes=64)
        b_rows = keep.tile([P, 8], F32, align_bytes=64)
        bias = keep.tile([P, M], F32, align_bytes=64)
        pre = {(h, i): keep.tile([P, HALF], F32, name="pre_%d_%d" % (h, i), align_bytes=64) for h in range(HALVES) for i in range(PACK)}
        res = {h: keep.tile([P, PACK, HALF], F32, name="res_%d" % h, align_bytes=64) for h in range(HALVES)}
        res_grouped = {h: keep.tile([P, HALF, PACK], BF16, name="res_grouped_%d" % h, align_bytes=64) for h in range(HALVES)}
        res_codes = {h: keep.tile([P, HALF], U32, name="res_codes_%d" % h, align_bytes=64) for h in range(HALVES)}
        res_scales = keep.tile([P, M], U8, align_bytes=64)

        def load_x(a):
            rows = x[a * P * PACK:(a + 1) * P * PACK, :].rearrange("(p j) t -> p j t", j=PACK)
            nc.sync.dma_start(out=x_raw[a][:], in_=rows)

        def load_w8(a, h):
            src = w8_words[a].rearrange("p n i -> p (n i)")[:, h * HALF * PACK:(h + 1) * HALF * PACK]
            nc.sync.dma_start(out=w8[a, h][:].bitcast(I32), in_=src.bitcast(I32))

        def load_w4(a, h0, h1):
            cols = slice(2 * HALF * h0, 2 * HALF * h1)
            nc.sync.dma_start(out=w4[a][:, cols].bitcast(I32), in_=w4_words[a][:, cols].bitcast(I32))

        def load_s8(h):
            for q in (0, 2, 1, 3):
                src = w8_scales[:, 4 * q:4 * q + 4, h * HALF:(h + 1) * HALF]
                nc.sync.dma_start(out=s8[h][32 * q:32 * q + 16, :].bitcast(I32), in_=src.bitcast(I32))

        def load_s4(plane, a0, a1):
            rows = w4_scales.rearrange("a (q r) n -> r q a n", r=4)
            for r in range(4):
                nc.sync.dma_start(out=plane[r:P:32, :, :].bitcast(I32), in_=rows[r][:, a0:a1, :].bitcast(I32))

        def group_views(f, a, c):
            dst = grouped[f, a][:, 2 * c:2 * c + 2, :, :].rearrange("p r m j -> p m j r")
            src = x_raw[a][:].rearrange("p j (m r) -> p m j r", r=PACK)[:, :, :, 2 * c:2 * c + 2]
            return dst, src

        def group_b(a, c):
            dst, src = group_views("b", a, c)
            nc.vector.tensor_copy(out=dst, in_=src)

        def group_a(a, c):
            dst, src = group_views("a", a, c)
            nc.scalar.activation(out=dst, in_=src, func=ACT.Square)

        def quantize(f, a, r0, r1):
            cols = slice(r0 * P, r1 * P)
            nc.vector.quantize_mx(
                out=codes[f, a][:, cols].bitcast(FP8X4),
                scales=scales[f, a][:, cols],
                in_=grouped[f, a][:, r0:r1, :, :].rearrange("p r m j -> p (r m j)"),
            )

        acc = {}
        done = {}

        def mm(f, a, h, i):
            if (h, i) not in acc:
                acc[h, i] = psum.tile([P, HALF], F32, name="acc_%d_%d" % (h, i), tag="bank_%d_%d" % (h, i))
                done[h, i] = 0
            cols = slice(i * P, (i + 1) * P)
            ncols = slice(h * HALF, (h + 1) * HALF)
            if f == "b":
                rhs = w8[a, h][:].bitcast(FP8X4)
                rhs_scale = s8[h][4 * a:, :]
            else:
                rhs = w4[a][:, 2 * h * HALF:2 * (h + 1) * HALF].bitcast(FP4X4)
                rhs_scale = s4_early[:, a, ncols] if a < PASSES - 1 else s4_last[:, 0, ncols]
            nc.tensor.matmul_mx(
                out=acc[h, i][:],
                lhsT=codes[f, a][:, cols].bitcast(FP8X4),
                lhsT_scale=scales[f, a][:, cols],
                rhs=rhs,
                rhs_scale=rhs_scale,
                start=(done[h, i] == 0),
                stop=(done[h, i] == 2 * PASSES - 1),
            )
            done[h, i] += 1

        def unit(f, a, h):
            for i in range(PACK):
                mm(f, a, h, i)

        out_rows = out_0.rearrange("(p i) n -> p i n", i=PACK)

        def add_bias(h, i, c0, c1):
            nc.vector.tensor_tensor(out=pre[h, i][:, c0:c1], in0=acc[h, i][:, c0:c1], in1=bias[:, h * HALF + c0:h * HALF + c1], op=ALU.add)

        def gelu(h, i, c0, c1):
            nc.scalar.activation(out=res[h][:, i, c0:c1], in_=pre[h, i][:, c0:c1], func=ACT.Gelu_apprx_tanh)

        def store_res(h, i):
            nc.sync.dma_start(out=out_rows[:, i, h * HALF:(h + 1) * HALF], in_=res[h][:, i, :])

        def group_res(h, c0, c1, on_vector):
            dst = res_grouped[h][:, c0:c1, :].rearrange("p (c u) i -> p c i u", u=4)
            src = res[h][:, :, c0:c1].rearrange("p i (c u) -> p c i u", u=4)
            if on_vector:
                nc.vector.tensor_copy(out=dst, in_=src)
            else:
                nc.scalar.copy(out=dst, in_=src)

        def quantize_res(h, c0, c1):
            nc.vector.quantize_mx(
                out=res_codes[h][:, c0:c1].bitcast(FP8X4),
                scales=res_scales[:, h * HALF + c0:h * HALF + c1],
                in_=res_grouped[h][:, c0:c1, :].rearrange("p n i -> p (n i)"),
            )

        def store_codes(h, c0, c1):
            dst = out_1[0].rearrange("p n i -> p (n i)")[:, (h * HALF + c0) * PACK:(h * HALF + c1) * PACK]
            nc.sync.dma_start(out=dst.bitcast(I32), in_=res_codes[h][:, c0:c1].bitcast(I32))

        def store_scales(q, queue):
            queue.dma_start(out=out_2[0, 4 * q:4 * q + 4, :].bitcast(I32), in_=res_scales[32 * q:32 * q + 4, :].bitcast(I32))

        nc.sync.dma_start(out=b_rows[:], in_=b.rearrange("(p c) -> p c", c=8))
        nc.vector.memset(s8[0][:].bitcast(I32), 0)
        nc.vector.memset(s4_early[:].rearrange("p a n -> p (a n)").bitcast(I32), 0)
        nc.vector.memset(s8[1][:].bitcast(I32), 0)
        nc.vector.memset(s4_last[:].rearrange("p a n -> p (a n)").bitcast(I32), 0)
        make_identity(nc, ident[:])

        load_x(0)
        load_s8(0)
        load_w8(0, 0)
        load_s4(s4_early, 0, PASSES - 1)
        load_w4(0, 0, 2)
        for a in range(1, PASSES):
            load_x(a)
            load_w8(a, 0)
            if a == PASSES - 1:
                load_s4(s4_last, a, a + 1)
            load_w4(a, 0, 2)
        load_s8(1)
        for a in range(PASSES):
            load_w8(a, 1)

        bias_banks = []
        for g in range(2):
            bank = psum.tile([P, 4, P], F32, name="bias_bank_%d" % g, tag="bank_1_%d" % (2 + g))
            for c in range(4):
                col = 4 * g + c
                nc.tensor.transpose(bank[:, c, :], b_rows[:, col:col + 1].to_broadcast([P, P]), ident[:])
            bias_banks.append(bank)

        def pair(f, a, h, c):
            for i in (2 * c, 2 * c + 1):
                mm(f, a, h, i)

        for c in range(CHUNKS):
            group_b(0, c)
            group_a(0, c)
            quantize("b", 0, 2 * c, 2 * c + 2)
            pair("b", 0, 0, c)
        for g in range(2):
            nc.scalar.copy(
                out=bias[:].rearrange("p (n g c) -> p n g c", g=2, c=4)[:, :, g, :],
                in_=bias_banks[g][:].rearrange("p c n -> p n c"),
            )
        for c in range(CHUNKS):
            quantize("a", 0, 2 * c, 2 * c + 2)
            pair("a", 0, 0, c)
            pair("a", 0, 1, c)
        for a in range(1, PASSES):
            for c in range(CHUNKS):
                group_b(a, c)
                group_a(a, c)
                quantize("b", a, 2 * c, 2 * c + 2)
                quantize("a", a, 2 * c, 2 * c + 2)
                pair("b", a, 0, c)
                pair("a", a, 0, c)
                pair("a", a, 1, c)
        for i in range(PACK):
            for a in range(PASSES):
                mm("b", a, 1, i)

        for i in range(PACK):
            add_bias(0, i, 0, HALF)
            gelu(0, i, 0, HALF)
            store_res(0, i)
        group_res(0, 384, 512, False)
        add_bias(1, 0, 0, HALF)
        gelu(1, 0, 0, HALF)
        store_res(1, 0)
        group_res(0, 0, 256, True)
        group_res(0, 256, 384, False)
        add_bias(1, 1, 0, HALF)
        gelu(1, 1, 0, HALF)
        store_res(1, 1)
        quantize_res(0, 0, 256)
        add_bias(1, 2, 0, HALF)
        gelu(1, 2, 0, HALF)
        quantize_res(0, 256, 512)
        store_codes(0, 0, HALF)
        store_res(1, 2)
        add_bias(1, 3, 0, 128)
        add_bias(1, 3, 128, 256)
        add_bias(1, 3, 256, 512)
        gelu(1, 3, 0, 128)
        gelu(1, 3, 128, 256)
        gelu(1, 3, 256, 512)
        store_res(1, 3)
        group_res(1, 0, 128, True)
        group_res(1, 128, 256, True)
        group_res(1, 384, 512, False)
        group_res(1, 256, 384, True)
        quantize_res(1, 0, 256)
        store_codes(1, 0, 256)
        quantize_res(1, 256, 512)
        store_codes(1, 256, 512)
        store_scales(0, nc.scalar)
        store_scales(2, nc.scalar)
        store_scales(1, nc.sync)
        store_scales(3, nc.sync)
